import numpy as np
import ml_dtypes

BF16 = ml_dtypes.bfloat16


def bf(x):
    return np.asarray(x, np.float32).astype(BF16)


def f32(x):
    return np.asarray(x, np.float32)


def f64(x):
    return np.asarray(x).astype(np.float64)


def striped(idx):
    return np.concatenate([l.reshape(-1, 16).T for l in idx])


def rows(idx, k):
    return np.tile(np.repeat(idx, 16, axis=0), (k // (16 * 8), 1))


def look(tab, idx):
    return np.take_along_axis(f64(tab), rows(idx, len(tab)), axis=1)


K, S, V, N = 256, 2048, 1536, 1536


def silu(v):
    return v / (1.0 + np.exp(-v))


def setup_inputs():
    return {"tab": f32(np.random.standard_normal((2, K, S))), "offs": striped(np.stack([np.random.permutation(S)[:N] for _ in range(8)]))}


def reference(tab, offs):
    idx = np.stack([g.T.reshape(-1) for g in np.split(offs, 8)])
    x = (np.minimum(np.maximum(look(tab[0], idx), -1.25), 1.0)) * (silu(look(tab[1], idx)))
    return x

@@ -1,0 +1,47 @@
+import concourse.mybir as mybir
+
+F32, U16 = mybir.dt.float32, mybir.dt.uint16
+P = 128
+PER_COLUMN = 16
+PIECE = 512
+LOW, HIGH = -1.25, 1.0
+
+
+def tile_lookup_vg_clipsilu_out_kernel(tc, tab, offs, out):
+    nc = tc.nc
+    rows, n = out.shape
+    places = tab.shape[2]
+    blocks, pieces = rows // P, n // PIECE
+    maximum, minimum, mult = mybir.AluOpType.max, mybir.AluOpType.min, mybir.AluOpType.mult
+    silu = mybir.ActivationFunctionType.Silu
+
+    with (
+        tc.tile_pool(name="lists", bufs=1) as list_pool,
+        tc.tile_pool(name="windows", bufs=blocks) as window_pool,
+        tc.tile_pool(name="work", bufs=blocks * pieces) as work_pool,
+    ):
+        offsets = list_pool.tile([P, n // PER_COLUMN], U16, name="offsets")
+        nc.sync.dma_start(offsets[:], offs)
+
+        values, gates = [], []
+        for b in range(blocks):
+            value = window_pool.tile([P, places], F32, name="value")
+            nc.sync.dma_start(value[:], tab[0, b * P : (b + 1) * P, :])
+            gate = window_pool.tile([P, places], F32, name="gate")
+            nc.sync.dma_start(gate[:], tab[1, b * P : (b + 1) * P, :])
+            values.append(value)
+            gates.append(gate)
+
+        step = PIECE // PER_COLUMN
+        for b in range(blocks):
+            for k in range(pieces):
+                piece_of_list = offsets[:, k * step : (k + 1) * step]
+                clamped = work_pool.tile([P, PIECE], F32, name="clamped")
+                nc.vector.tensor_scalar(
+                    clamped[:], values[b][:].indirect(piece_of_list), LOW, HIGH, maximum, minimum
+                )
+                activated = work_pool.tile([P, PIECE], F32, name="activated")
+                nc.scalar.activation(activated[:], gates[b][:].indirect(piece_of_list), silu)
+                x = work_pool.tile([P, PIECE], F32, name="x")
+                nc.vector.tensor_tensor(x[:], clamped[:], activated[:], mult)
+                nc.sync.dma_start(out[b * P : (b + 1) * P, k * PIECE : (k + 1) * PIECE], x[:])

@@ -32,6 +32,11 @@ def tile_lookup_vg_clipsilu_out_kernel(tc, tab, offs, out):
             values.append(value)
             gates.append(gate)
 
+        zeros = list_pool.tile([P, 1], F32, name="zeros")
+        nc.gpsimd.memset(zeros[:], 0.0)
+        warmed = list_pool.tile([P, 1], F32, name="warmed")
+        nc.scalar.activation(warmed[:], zeros[:], silu)
+
         step = PIECE // PER_COLUMN
         for b in range(blocks):
             for k in range(pieces):

@@ -19,6 +19,7 @@ def tile_lookup_vg_clipsilu_out_kernel(tc, tab, offs, out):
         tc.tile_pool(name="lists", bufs=1) as list_pool,
         tc.tile_pool(name="windows", bufs=blocks) as window_pool,
         tc.tile_pool(name="work", bufs=blocks * pieces) as work_pool,
+        tc.tile_pool(name="products", bufs=2 * blocks * pieces) as x_pool,
     ):
         offsets = list_pool.tile([P, n // PER_COLUMN], U16, name="offsets")
         nc.sync.dma_start(offsets[:], offs)
@@ -39,6 +40,9 @@ def tile_lookup_vg_clipsilu_out_kernel(tc, tab, offs, out):
 
         step = PIECE // PER_COLUMN
         for b in range(blocks):
+            last = b == blocks - 1
+            multiplier = nc.vector if last else nc.gpsimd
+            width = PIECE // 2 if last else PIECE
             for k in range(pieces):
                 piece_of_list = offsets[:, k * step : (k + 1) * step]
                 clamped = work_pool.tile([P, PIECE], F32, name="clamped")
@@ -47,6 +51,9 @@ def tile_lookup_vg_clipsilu_out_kernel(tc, tab, offs, out):
                 )
                 activated = work_pool.tile([P, PIECE], F32, name="activated")
                 nc.scalar.activation(activated[:], gates[b][:].indirect(piece_of_list), silu)
-                x = work_pool.tile([P, PIECE], F32, name="x")
-                nc.vector.tensor_tensor(x[:], clamped[:], activated[:], mult)
-                nc.sync.dma_start(out[b * P : (b + 1) * P, k * PIECE : (k + 1) * PIECE], x[:])
+                for first in range(0, PIECE, width):
+                    part = slice(first, first + width)
+                    x = x_pool.tile([P, width], F32, name="x")
+                    multiplier.tensor_tensor(x[:], clamped[:, part], activated[:, part], mult)
+                    column = k * PIECE + first
+                    nc.sync.dma_start(out[b * P : (b + 1) * P, column : column + width], x[:])

import concourse.mybir as mybir

F32, U16 = mybir.dt.float32, mybir.dt.uint16
P = 128
PER_COLUMN = 16
PIECE = 512
LOW, HIGH = -1.25, 1.0


def tile_lookup_vg_clipsilu_out_kernel(tc, tab, offs, out):
    nc = tc.nc
    rows, n = out.shape
    places = tab.shape[2]
    blocks, pieces = rows // P, n // PIECE
    maximum, minimum, mult = mybir.AluOpType.max, mybir.AluOpType.min, mybir.AluOpType.mult
    silu = mybir.ActivationFunctionType.Silu

    with (
        tc.tile_pool(name="lists", bufs=1) as list_pool,
        tc.tile_pool(name="windows", bufs=blocks) as window_pool,
        tc.tile_pool(name="work", bufs=blocks * pieces) as work_pool,
        tc.tile_pool(name="products", bufs=2 * blocks * pieces) as x_pool,
    ):
        offsets = list_pool.tile([P, n // PER_COLUMN], U16, name="offsets")
        nc.sync.dma_start(offsets[:], offs)

        values, gates = [], []
        for b in range(blocks):
            value = window_pool.tile([P, places], F32, name="value")
            nc.sync.dma_start(value[:], tab[0, b * P : (b + 1) * P, :])
            gate = window_pool.tile([P, places], F32, name="gate")
            nc.sync.dma_start(gate[:], tab[1, b * P : (b + 1) * P, :])
            values.append(value)
            gates.append(gate)

        zeros = list_pool.tile([P, 1], F32, name="zeros")
        nc.gpsimd.memset(zeros[:], 0.0)
        warmed = list_pool.tile([P, 1], F32, name="warmed")
        nc.scalar.activation(warmed[:], zeros[:], silu)

        step = PIECE // PER_COLUMN
        for b in range(blocks):
            last = b == blocks - 1
            multiplier = nc.vector if last else nc.gpsimd
            width = PIECE // 2 if last else PIECE
            for k in range(pieces):
                piece_of_list = offsets[:, k * step : (k + 1) * step]
                clamped = work_pool.tile([P, PIECE], F32, name="clamped")
                nc.vector.tensor_scalar(
                    clamped[:], values[b][:].indirect(piece_of_list), LOW, HIGH, maximum, minimum
                )
                activated = work_pool.tile([P, PIECE], F32, name="activated")
                nc.scalar.activation(activated[:], gates[b][:].indirect(piece_of_list), silu)
                for first in range(0, PIECE, width):
                    part = slice(first, first + width)
                    x = x_pool.tile([P, width], F32, name="x")
                    multiplier.tensor_tensor(x[:], clamped[:, part], activated[:, part], mult)
                    column = k * PIECE + first
                    nc.sync.dma_start(out[b * P : (b + 1) * P, column : column + width], x[:])
